import numpy as np
import ml_dtypes


def mxq(x, axis, fmt="e4m3"):
    dtype, down = {"e4m3": (ml_dtypes.float8_e4m3fn, 7), "e5m2": (ml_dtypes.float8_e5m2, 14)}[fmt]
    v = np.moveaxis(np.asarray(x, np.float32).astype(ml_dtypes.bfloat16).astype(np.float64), axis, -1)
    blocks = v.reshape(v.shape[:-1] + (-1, 32))
    amax = np.abs(blocks).max(-1, keepdims=True)
    byte = np.maximum(np.where(amax > 0, np.frexp(amax)[1] - 1 + 127, 0) - down, 1)
    scale = np.exp2(byte - 127.0)
    codes = (blocks / scale).astype(np.float32).astype(dtype).astype(np.float64)
    return np.moveaxis((codes * scale).reshape(v.shape), -1, axis)


WIDE = False


def mx_kscale(k):
    if not WIDE:
        return np.ones(k)
    levels = np.array([10, -10, 5, -5, 0])
    if k % 512:
        return np.exp2(np.random.permutation(np.resize(levels, k // 32))).repeat(32)
    a = np.empty((k // 512, 16))
    for p in range(k // 512):
        a[p, :8] = np.random.permutation(np.resize(levels, 8))
        for g in range(8):
            far = levels[np.abs(levels - a[p, g]) >= 10]
            a[p, g + 8] = far[np.random.randint(len(far))]
    return np.exp2(a.ravel()).repeat(32)


def f64(x):
    return np.asarray(x).astype(np.float64)


def striped(idx):
    return np.tile(idx.reshape(-1, 16).T, (8, 1)).astype(np.uint16)


def unstriped(offs):
    return offs[:16].T.reshape(-1).astype(np.int64)


E2M1 = np.array([0.0, 0.5, 1.0, 1.5, 2.0, 3.0, 4.0, 6.0, -0.0, -0.5, -1.0, -1.5, -2.0, -3.0, -4.0, -6.0])


def pack_weight(w, fmt):
    k, n = w.shape
    w = f64(np.asarray(w, np.float32).astype(ml_dtypes.bfloat16)).reshape(k // 32, 32, n)
    amax = np.abs(w).max(1)
    if fmt == "e4m3":
        byte = np.frexp(amax)[1] - 1 + 127 - 7
    else:
        mant, ex = np.frexp(amax / 6.0)
        byte = np.where(mant > 0.5, ex, ex - 1) + 127
    byte = np.clip(np.where(amax > 0, byte, 1), 1, 254)
    scaled = (w * np.exp2(127.0 - byte)[:, None, :]).reshape(k, n).astype(np.float32)
    by_word = np.ascontiguousarray(scaled.reshape(k // 512, 128, 4, n).transpose(0, 1, 3, 2))
    if fmt == "e4m3":
        words = by_word.astype(ml_dtypes.float8_e4m3fn).view(np.uint8)
    else:
        c = by_word.astype(ml_dtypes.float4_e2m1fn).view(np.uint8) & 0xF
        words = (c[..., 0::2] | (c[..., 1::2] << 4)).reshape(k // 512, 128, 2 * n)
    return np.ascontiguousarray(words), np.ascontiguousarray(byte.astype(np.uint8).reshape(k // 512, 16, n))


def unpack_weight(words, scales, fmt):
    g, _, n = scales.shape
    words = np.ascontiguousarray(words).reshape(g, 128, n, -1)
    if fmt == "e4m3":
        vals = words.view(ml_dtypes.float8_e4m3fn).astype(np.float64)
    else:
        nib = np.empty((g, 128, n, 4), np.uint8)
        nib[..., 0::2] = words & 0xF
        nib[..., 1::2] = words >> 4
        vals = E2M1[nib]
    vals = vals * np.repeat(np.exp2(scales.astype(np.float64) - 127.0), 8, axis=1)[..., None]
    return vals.transpose(0, 1, 3, 2).reshape(g * 512, n)


def relu(v):
    return np.maximum(v, 0.0)


K, T, E, B, H, N = 512, 1024, 4, 6, 512, 256


def setup_inputs():
    n = np.random.standard_normal
    s = mx_kscale(K)
    u = mx_kscale(H)
    slot_token = np.random.permutation(T)[:128 * B]
    block = np.sort(np.random.randint(E, size=B))
    x = pack_weight(n((K, T)) * s[:, None], "e4m3")
    w = pack_weight(n((K, N)) / np.sqrt(K) / s[:, None], "e4m3")
    wa = pack_weight(n((K, E * H)) / np.sqrt(K) / s[:, None] * np.tile(u, E), "e4m3")
    wb = pack_weight(n((H, E * N)) / np.sqrt(H) / u[:, None], "e4m3")
    return {
        "x_words": x[0],
        "x_scales": x[1],
        "w_words": w[0],
        "w_scales": w[1],
        "wa_words": wa[0],
        "wa_scales": wa[1],
        "wb_words": wb[0],
        "wb_scales": wb[1],
        "gate": (np.tile(np.random.uniform(0.2, 1.0, 128 * B), (128, 1))).astype(np.float32),
        "offs": striped(slot_token),
        "offs2": striped((block[:, None] * H + np.arange(H)).reshape(-1)),
        "offs3": striped((block[:, None] * N + np.arange(N)).reshape(-1)),
    }


def reference(x_words, x_scales, w_words, w_scales, wa_words, wa_scales, wb_words, wb_scales, gate, offs, offs2, offs3):
    w = unpack_weight(w_words, w_scales, "e4m3")
    idx, idx2, idx3 = unstriped(offs), unstriped(offs2), unstriped(offs3)
    x = unpack_weight(x_words, x_scales, "e4m3")
    out = w.T @ x
    wa = unpack_weight(wa_words, wa_scales, "e4m3")[:, idx2]
    wb = unpack_weight(wb_words, wb_scales, "e4m3")[:, idx3]
    xq = x[:, idx]
    h = np.concatenate([wa[:, m * H:(m + 1) * H].T @ xq[:, 128 * m:128 * m + 128] for m in range(B)], axis=1)
    hq = mxq(relu(h), 0, "e4m3")
    y = np.concatenate([wb[:, m * N:(m + 1) * N].T @ hq[:, 128 * m:128 * m + 128] for m in range(B)], axis=1)
    out[:, idx] += f64(gate[:1]) * y
    return out

@@ -1,0 +1,180 @@
+from contextlib import ExitStack
+
+import concourse.mybir as mybir
+from concourse.masks import make_identity
+
+K, T, E, B, H, N = 512, 1024, 4, 6, 512, 256
+FLOPS = 2 * K * N * T + 2 * 128 * B * (K * H + H * N)
+
+F32 = mybir.dt.float32
+BF16 = mybir.dt.bfloat16
+I32 = mybir.dt.int32
+U32 = mybir.dt.uint32
+U16 = mybir.dt.uint16
+U8 = mybir.dt.uint8
+FP8X4 = mybir.dt.float8_e4m3fn_x4
+ACT = mybir.ActivationFunctionType
+
+P = 128
+SLOTS = P * B
+PAIRS = B // 2
+BANK = 512
+HALVES = N // P
+
+
+def tile_moe_dyl_relu_kernel(
+    tc, x_words, x_scales, w_words, w_scales, wa_words, wa_scales, wb_words, wb_scales, gate, offs, offs2, offs3, out
+):
+    nc = tc.nc
+    with ExitStack() as ctx:
+        keep = ctx.enter_context(tc.tile_pool(name="keep", bufs=1))
+        psum = ctx.enter_context(tc.psum_pool(name="psum", bufs=1))
+
+        def held(name, shape, dtype):
+            return keep.tile(shape, dtype, name=name, align_bytes=64)
+
+        def plane(name, width):
+            tile = held(name, [P, width], U8)
+            nc.vector.memset(tile[:].bitcast(I32), 0)
+            return tile
+
+        def load_plane(queue, tile, scales):
+            for q in range(4):
+                queue.dma_start(tile[32 * q : 32 * q + 4, :].bitcast(I32), scales[0, 4 * q : 4 * q + 4, :].bitcast(I32))
+
+        def load_words(name, words):
+            tile = held(name, [P, words.shape[2]], I32)
+            nc.sync.dma_start(tile[:], words[0].rearrange("p c d -> p (c d)").bitcast(I32))
+            return tile
+
+        def load_list(name, source):
+            tile = held(name, [P, source.shape[1]], U16)
+            nc.sync.dma_start(tile[:], source)
+            return tile
+
+        def mx(result, a_words, a_scales, b_words, b_scales):
+            nc.tensor.matmul_mx(
+                out=result, lhsT=a_words.bitcast(FP8X4), lhsT_scale=a_scales,
+                rhs=b_words.bitcast(FP8X4), rhs_scale=b_scales, start=True, stop=True,
+            )
+
+        def gather(name, window, dtype, offsets, first, count):
+            tile = held(name, [P, count], dtype)
+            picked = offsets[:, first // 16 : (first + count) // 16]
+            nc.vector.tensor_copy(tile[:], window[:].bitcast(dtype).indirect(picked))
+            return tile
+
+        ident = held("ident", [P, P], F32)
+        make_identity(nc, ident[:])
+
+        xs = plane("xs", T)
+        was = plane("was", E * H)
+        ws = plane("ws", N)
+        wbs = plane("wbs", E * N)
+
+        tokens = load_list("tokens", offs)
+        xw = load_words("xw", x_words)
+        load_plane(nc.scalar, xs, x_scales)
+        cols_a = load_list("cols_a", offs2)
+        waw = load_words("waw", wa_words)
+        load_plane(nc.scalar, was, wa_scales)
+        ww = load_words("ww", w_words)
+        load_plane(nc.gpsimd, ws, w_scales)
+        cols_b = load_list("cols_b", offs3)
+        wbw = load_words("wbw", wb_words)
+        load_plane(nc.gpsimd, wbs, wb_scales)
+        gate_col = held("gate_col", [P, B], F32)
+        with nc.allow_non_contiguous_dma(reason="one gate value a partition"):
+            nc.sync.dma_start(gate_col[:], gate[0:1, :].rearrange("o (m p) -> p (o m)", p=P))
+
+        xgw = gather("xgw", xw, U32, tokens, 0, SLOTS)
+        xgs = gather("xgs", xs, U8, tokens, 0, SLOTS)
+
+        result = [held("result%d" % c, [P, T], F32) for c in range(HALVES)]
+        for c in range(HALVES):
+            rows = slice(c * P, (c + 1) * P)
+            for t0 in range(0, T, BANK):
+                cols = slice(t0, t0 + BANK)
+                acc = psum.tile([P, BANK], F32, tag="work", bufs=3, name="base")
+                mx(acc[:], ww[:, rows], ws[:, rows], xw[:, cols], xs[:, cols])
+                nc.scalar.activation(result[c][:, cols], acc[:], ACT.Copy)
+
+        sums = []
+        for pair in range(PAIRS):
+            acc = psum.tile([P, 2, N], F32, tag="work", bufs=3, name="slot_base")
+            for b in range(2):
+                slots = slice((2 * pair + b) * P, (2 * pair + b + 1) * P)
+                mx(acc[:, b, :], xgw[:, slots], xgs[:, slots], ww[:], ws[:])
+            staged = held("slot_base%d" % pair, [P, 2, N], F32)
+            nc.scalar.copy(staged[:], acc[:])
+            total = psum.tile([P, HALVES, 2, P], F32, name="total%d" % pair)
+            for b in range(2):
+                for c in range(HALVES):
+                    nc.tensor.matmul(
+                        total[:, c, b, :], staged[:, b, c * P : (c + 1) * P], ident[:],
+                        start=(b == 0 and c == 0), stop=False, is_transpose=True,
+                    )
+            sums.append(total)
+
+        grouped = []
+        for pair in range(PAIRS):
+            ags = gather("ags%d" % pair, was, U8, cols_a, 2 * pair * H, 2 * H)
+            agw = gather("agw%d" % pair, waw, U32, cols_a, 2 * pair * H, 2 * H)
+            turned = psum.tile([P, 2, 2, P], F32, tag="work", bufs=3, name="turned")
+            for b in range(2):
+                slots = slice((2 * pair + b) * P, (2 * pair + b + 1) * P)
+                inner = slice(b * H, (b + 1) * H)
+                acc = psum.tile([P, H], F32, tag="hidden", bufs=2, name="hidden")
+                mx(acc[:], xgw[:, slots], xgs[:, slots], agw[:, inner], ags[:, inner])
+                h = held("h%d" % (2 * pair + b), [P, H], BF16)
+                nc.scalar.activation(
+                    h[:].rearrange("j (u p e) -> j u p e", u=2, e=2),
+                    acc[:].rearrange("j (p u e) -> j u p e", u=2, e=2),
+                    ACT.Relu,
+                )
+                for u in range(2):
+                    nc.tensor.transpose(turned[:, b, u, :], h[:].bitcast(F32)[:, u * P : (u + 1) * P], ident[:])
+            hg = held("hg%d" % pair, [P, 2 * P * 4], BF16)
+            nc.scalar.copy(
+                hg[:].bitcast(F32).rearrange("p (b j u) -> p b j u", b=2, u=2),
+                turned[:].rearrange("p b u j -> p b j u"),
+            )
+            grouped.append(hg)
+
+        values = held("values", [P, HALVES, SLOTS], F32)
+        for pair in range(PAIRS):
+            bgs = gather("bgs%d" % pair, wbs, U8, cols_b, 2 * pair * N, 2 * N)
+            bgw = gather("bgw%d" % pair, wbw, U32, cols_b, 2 * pair * N, 2 * N)
+            hw = held("hw%d" % pair, [P, 2 * P], U32)
+            hs = held("hs%d" % pair, [P, 2 * P], U8)
+            nc.vector.quantize_mx(out=hw[:].bitcast(FP8X4), scales=hs[:], in_=grouped[pair][:])
+            acc = psum.tile([P, 2, N], F32, tag="work", bufs=3, name="y")
+            gated = held("gated%d" % pair, [P, 2, N], F32)
+            for b in range(2):
+                mx(acc[:, b, :], hw[:, b * P : (b + 1) * P], hs[:, b * P : (b + 1) * P],
+                   bgw[:, b * N : (b + 1) * N], bgs[:, b * N : (b + 1) * N])
+            for b in range(2):
+                m = 2 * pair + b
+                nc.scalar.activation(gated[:, b, :], acc[:, b, :], ACT.Copy, scale=gate_col[:, m : m + 1])
+            for b in range(2):
+                for c in range(HALVES):
+                    nc.tensor.matmul(
+                        sums[pair][:, c, b, :], gated[:, b, c * P : (c + 1) * P], ident[:],
+                        start=False, stop=(b == 1 and c == HALVES - 1), is_transpose=True,
+                    )
+            nc.scalar.copy(
+                values[:, :, 2 * pair * P : 2 * (pair + 1) * P],
+                sums[pair][:].rearrange("n c b j -> n c (b j)"),
+            )
+
+        def scatter(c, first, count):
+            picked = tokens[:, first // 16 : (first + count) // 16]
+            nc.vector.tensor_copy(result[c][:].indirect(picked), values[:, c, first : first + count])
+
+        scatter(1, 0, 2 * P)
+        for pair in range(PAIRS):
+            scatter(0, 2 * pair * P, 2 * P)
+        nc.sync.dma_start(out[0:P, :], result[0][:])
+        scatter(1, 2 * P, 4 * P)
+        nc.sync.dma_start(out[P:N, 0:BANK], result[1][:, 0:BANK])
+        nc.scalar.dma_start(out[P:N, BANK:T], result[1][:, BANK:T])

@@ -67,28 +67,31 @@ def tile_moe_dyl_relu_kernel(
         ident = held("ident", [P, P], F32)
         make_identity(nc, ident[:])
 
-        xs = plane("xs", T)
-        was = plane("was", E * H)
         ws = plane("ws", N)
+        was = plane("was", E * H)
         wbs = plane("wbs", E * N)
 
         tokens = load_list("tokens", offs)
+        xs = held("xs", [P, T], U8)
+        for q in range(4):
+            rows = x_scales[0, 4 * q : 4 * q + 4, :].bitcast(I32)
+            nc.sync.dma_start(xs[32 * q : 32 * q + 32, :].bitcast(I32), rows.unsqueeze(0).to_broadcast([8, 4, T // 4]))
         xw = load_words("xw", x_words)
-        load_plane(nc.scalar, xs, x_scales)
         cols_a = load_list("cols_a", offs2)
-        waw = load_words("waw", wa_words)
-        load_plane(nc.scalar, was, wa_scales)
+        load_plane(nc.sync, ws, w_scales)
         ww = load_words("ww", w_words)
-        load_plane(nc.gpsimd, ws, w_scales)
+        load_plane(nc.sync, was, wa_scales)
+        waw = load_words("waw", wa_words)
         cols_b = load_list("cols_b", offs3)
         wbw = load_words("wbw", wb_words)
-        load_plane(nc.gpsimd, wbs, wb_scales)
+        load_plane(nc.sync, wbs, wb_scales)
         gate_col = held("gate_col", [P, B], F32)
         with nc.allow_non_contiguous_dma(reason="one gate value a partition"):
             nc.sync.dma_start(gate_col[:], gate[0:1, :].rearrange("o (m p) -> p (o m)", p=P))
 
-        xgw = gather("xgw", xw, U32, tokens, 0, SLOTS)
         xgs = gather("xgs", xs, U8, tokens, 0, SLOTS)
+        xgw = gather("xgw", xw, U32, tokens, 0, SLOTS)
+        early = [gather("ags%d" % pair, was, U8, cols_a, 2 * pair * H, 2 * H) for pair in range(PAIRS - 1)]
 
         result = [held("result%d" % c, [P, T], F32) for c in range(HALVES)]
         for c in range(HALVES):
@@ -118,7 +121,7 @@ def tile_moe_dyl_relu_kernel(
 
         grouped = []
         for pair in range(PAIRS):
-            ags = gather("ags%d" % pair, was, U8, cols_a, 2 * pair * H, 2 * H)
+            ags = early[pair] if pair < len(early) else gather("ags%d" % pair, was, U8, cols_a, 2 * pair * H, 2 * H)
             agw = gather("agw%d" % pair, waw, U32, cols_a, 2 * pair * H, 2 * H)
             turned = psum.tile([P, 2, 2, P], F32, tag="work", bufs=3, name="turned")
             for b in range(2):
@@ -143,8 +146,8 @@ def tile_moe_dyl_relu_kernel(
 
         values = held("values", [P, HALVES, SLOTS], F32)
         for pair in range(PAIRS):
-            bgs = gather("bgs%d" % pair, wbs, U8, cols_b, 2 * pair * N, 2 * N)
             bgw = gather("bgw%d" % pair, wbw, U32, cols_b, 2 * pair * N, 2 * N)
+            bgs = gather("bgs%d" % pair, wbs, U8, cols_b, 2 * pair * N, 2 * N)
             hw = held("hw%d" % pair, [P, 2 * P], U32)
             hs = held("hs%d" % pair, [P, 2 * P], U8)
             nc.vector.quantize_mx(out=hw[:].bitcast(FP8X4), scales=hs[:], in_=grouped[pair][:])

@@ -30,8 +30,8 @@ def tile_moe_dyl_relu_kernel(
         keep = ctx.enter_context(tc.tile_pool(name="keep", bufs=1))
         psum = ctx.enter_context(tc.psum_pool(name="psum", bufs=1))
 
-        def held(name, shape, dtype):
-            return keep.tile(shape, dtype, name=name, align_bytes=64)
+        def held(name, shape, dtype, tag=None, bufs=1):
+            return keep.tile(shape, dtype, name=name, tag=tag or name, bufs=bufs, align_bytes=64)
 
         def plane(name, width):
             tile = held(name, [P, width], U8)
@@ -58,8 +58,8 @@ def tile_moe_dyl_relu_kernel(
                 rhs=b_words.bitcast(FP8X4), rhs_scale=b_scales, start=True, stop=True,
             )
 
-        def gather(name, window, dtype, offsets, first, count):
-            tile = held(name, [P, count], dtype)
+        def gather(name, window, dtype, offsets, first, count, tag=None, bufs=1):
+            tile = held(name, [P, count], dtype, tag, bufs)
             picked = offsets[:, first // 16 : (first + count) // 16]
             nc.vector.tensor_copy(tile[:], window[:].bitcast(dtype).indirect(picked))
             return tile
@@ -67,20 +67,21 @@ def tile_moe_dyl_relu_kernel(
         ident = held("ident", [P, P], F32)
         make_identity(nc, ident[:])
 
-        ws = plane("ws", N)
         was = plane("was", E * H)
+        ws = plane("ws", N)
         wbs = plane("wbs", E * N)
 
         tokens = load_list("tokens", offs)
         xs = held("xs", [P, T], U8)
         for q in range(4):
             rows = x_scales[0, 4 * q : 4 * q + 4, :].bitcast(I32)
-            nc.sync.dma_start(xs[32 * q : 32 * q + 32, :].bitcast(I32), rows.unsqueeze(0).to_broadcast([8, 4, T // 4]))
+            queue = nc.sync if q < 2 else nc.scalar
+            queue.dma_start(xs[32 * q : 32 * q + 32, :].bitcast(I32), rows.unsqueeze(0).to_broadcast([8, 4, T // 4]))
         xw = load_words("xw", x_words)
         cols_a = load_list("cols_a", offs2)
-        load_plane(nc.sync, ws, w_scales)
-        ww = load_words("ww", w_words)
         load_plane(nc.sync, was, wa_scales)
+        ww = load_words("ww", w_words)
+        load_plane(nc.sync, ws, w_scales)
         waw = load_words("waw", wa_words)
         cols_b = load_list("cols_b", offs3)
         wbw = load_words("wbw", wb_words)
@@ -91,7 +92,6 @@ def tile_moe_dyl_relu_kernel(
 
         xgs = gather("xgs", xs, U8, tokens, 0, SLOTS)
         xgw = gather("xgw", xw, U32, tokens, 0, SLOTS)
-        early = [gather("ags%d" % pair, was, U8, cols_a, 2 * pair * H, 2 * H) for pair in range(PAIRS - 1)]
 
         result = [held("result%d" % c, [P, T], F32) for c in range(HALVES)]
         for c in range(HALVES):
@@ -119,10 +119,13 @@ def tile_moe_dyl_relu_kernel(
                     )
             sums.append(total)
 
-        grouped = []
-        for pair in range(PAIRS):
-            ags = early[pair] if pair < len(early) else gather("ags%d" % pair, was, U8, cols_a, 2 * pair * H, 2 * H)
-            agw = gather("agw%d" % pair, waw, U32, cols_a, 2 * pair * H, 2 * H)
+        values = held("values", [P, HALVES, SLOTS], F32)
+
+        def first_scales(pair):
+            return gather("ags%d" % pair, was, U8, cols_a, 2 * pair * H, 2 * H, "ags", 2)
+
+        def first_layer(pair, ags):
+            agw = gather("agw%d" % pair, waw, U32, cols_a, 2 * pair * H, 2 * H, "hg0" if pair == 2 else None)
             turned = psum.tile([P, 2, 2, P], F32, tag="work", bufs=3, name="turned")
             for b in range(2):
                 slots = slice((2 * pair + b) * P, (2 * pair + b + 1) * P)
@@ -142,15 +145,17 @@ def tile_moe_dyl_relu_kernel(
                 hg[:].bitcast(F32).rearrange("p (b j u) -> p b j u", b=2, u=2),
                 turned[:].rearrange("p b u j -> p b j u"),
             )
-            grouped.append(hg)
+            return hg
 
-        values = held("values", [P, HALVES, SLOTS], F32)
-        for pair in range(PAIRS):
-            bgw = gather("bgw%d" % pair, wbw, U32, cols_b, 2 * pair * N, 2 * N)
-            bgs = gather("bgs%d" % pair, wbs, U8, cols_b, 2 * pair * N, 2 * N)
+        def second_matrices(pair):
+            bgw = gather("bgw%d" % pair, wbw, U32, cols_b, 2 * pair * N, 2 * N, "bgw", 2)
+            bgs = gather("bgs%d" % pair, wbs, U8, cols_b, 2 * pair * N, 2 * N, "bgs", 2)
+            return bgw, bgs
+
+        def second_layer(pair, hg, bgw, bgs):
             hw = held("hw%d" % pair, [P, 2 * P], U32)
             hs = held("hs%d" % pair, [P, 2 * P], U8)
-            nc.vector.quantize_mx(out=hw[:].bitcast(FP8X4), scales=hs[:], in_=grouped[pair][:])
+            nc.vector.quantize_mx(out=hw[:].bitcast(FP8X4), scales=hs[:], in_=hg[:])
             acc = psum.tile([P, 2, N], F32, tag="work", bufs=3, name="y")
             gated = held("gated%d" % pair, [P, 2, N], F32)
             for b in range(2):
@@ -165,19 +170,34 @@ def tile_moe_dyl_relu_kernel(
                         sums[pair][:, c, b, :], gated[:, b, c * P : (c + 1) * P], ident[:],
                         start=False, stop=(b == 1 and c == HALVES - 1), is_transpose=True,
                     )
-            nc.scalar.copy(
-                values[:, :, 2 * pair * P : 2 * (pair + 1) * P],
-                sums[pair][:].rearrange("n c b j -> n c (b j)"),
-            )
+            for c in range(HALVES):
+                nc.scalar.copy(
+                    values[:, c, 2 * pair * P : 2 * (pair + 1) * P],
+                    sums[pair][:, c, :, :].rearrange("n b j -> n (b j)"),
+                )
 
-        def scatter(c, first, count):
+        def scatter(pair, c):
+            first, count = 2 * pair * P, 2 * P
             picked = tokens[:, first // 16 : (first + count) // 16]
             nc.vector.tensor_copy(result[c][:].indirect(picked), values[:, c, first : first + count])
 
-        scatter(1, 0, 2 * P)
-        for pair in range(PAIRS):
-            scatter(0, 2 * pair * P, 2 * P)
+        ags0 = first_scales(0)
+        ags1 = first_scales(1)
+        hg0 = first_layer(0, ags0)
+        hg1 = first_layer(1, ags1)
+        second0 = second_matrices(0)
+        ags2 = first_scales(2)
+        second1 = second_matrices(1)
+        second_layer(0, hg0, *second0)
+        hg2 = first_layer(2, ags2)
+        second_layer(1, hg1, *second1)
+        second2 = second_matrices(2)
+        scatter(0, 0)
+        second_layer(2, hg2, *second2)
+        scatter(0, 1)
+        for pair in range(1, PAIRS):
+            for c in range(HALVES):
+                scatter(pair, c)
         nc.sync.dma_start(out[0:P, :], result[0][:])
-        scatter(1, 2 * P, 4 * P)
         nc.sync.dma_start(out[P:N, 0:BANK], result[1][:, 0:BANK])
         nc.scalar.dma_start(out[P:N, BANK:T], result[1][:, BANK:T])

@@ -39,8 +39,8 @@ def tile_moe_dyl_relu_kernel(
             return tile
 
         def load_plane(queue, tile, scales):
-            for q in range(4):
-                queue.dma_start(tile[32 * q : 32 * q + 4, :].bitcast(I32), scales[0, 4 * q : 4 * q + 4, :].bitcast(I32))
+            for r in range(4):
+                queue.dma_start(tile[r:P:32, :].bitcast(I32), scales[0, r:16:4, :].bitcast(I32))
 
         def load_words(name, words):
             tile = held(name, [P, words.shape[2]], I32)
@@ -75,7 +75,7 @@ def tile_moe_dyl_relu_kernel(
         xs = held("xs", [P, T], U8)
         for q in range(4):
             rows = x_scales[0, 4 * q : 4 * q + 4, :].bitcast(I32)
-            queue = nc.sync if q < 2 else nc.scalar
+            queue = nc.scalar if q < 2 else nc.sync
             queue.dma_start(xs[32 * q : 32 * q + 32, :].bitcast(I32), rows.unsqueeze(0).to_broadcast([8, 4, T // 4]))
         xw = load_words("xw", x_words)
         cols_a = load_list("cols_a", offs2)
@@ -94,23 +94,25 @@ def tile_moe_dyl_relu_kernel(
         xgw = gather("xgw", xw, U32, tokens, 0, SLOTS)
 
         result = [held("result%d" % c, [P, T], F32) for c in range(HALVES)]
-        for c in range(HALVES):
+
+        def frozen_layer(c):
             rows = slice(c * P, (c + 1) * P)
             for t0 in range(0, T, BANK):
                 cols = slice(t0, t0 + BANK)
-                acc = psum.tile([P, BANK], F32, tag="work", bufs=3, name="base")
+                acc = psum.tile([P, BANK], F32, tag="hidden", bufs=2, name="base")
                 mx(acc[:], ww[:, rows], ws[:, rows], xw[:, cols], xs[:, cols])
                 nc.scalar.activation(result[c][:, cols], acc[:], ACT.Copy)
 
+        frozen_layer(0)
         sums = []
         for pair in range(PAIRS):
-            acc = psum.tile([P, 2, N], F32, tag="work", bufs=3, name="slot_base")
+            acc = psum.tile([P, 2, N], F32, tag="work", bufs=2, name="slot_base")
             for b in range(2):
                 slots = slice((2 * pair + b) * P, (2 * pair + b + 1) * P)
                 mx(acc[:, b, :], xgw[:, slots], xgs[:, slots], ww[:], ws[:])
             staged = held("slot_base%d" % pair, [P, 2, N], F32)
             nc.scalar.copy(staged[:], acc[:])
-            total = psum.tile([P, HALVES, 2, P], F32, name="total%d" % pair)
+            total = psum.tile([P, HALVES, 2, P], F32, tag="total%d" % pair, bufs=1, name="total")
             for b in range(2):
                 for c in range(HALVES):
                     nc.tensor.matmul(
@@ -118,20 +120,28 @@ def tile_moe_dyl_relu_kernel(
                         start=(b == 0 and c == 0), stop=False, is_transpose=True,
                     )
             sums.append(total)
+        frozen_layer(1)
 
         values = held("values", [P, HALVES, SLOTS], F32)
 
-        def first_scales(pair):
-            return gather("ags%d" % pair, was, U8, cols_a, 2 * pair * H, 2 * H, "ags", 2)
+        def first_scales(trio):
+            return gather("ags%d" % trio, was, U8, cols_a, 3 * trio * H, 3 * H)
+
+        def second_scales(trio):
+            return gather("bgs%d" % trio, wbs, U8, cols_b, 3 * trio * N, 3 * N, "hs0" if trio == 1 else None)
 
         def first_layer(pair, ags):
             agw = gather("agw%d" % pair, waw, U32, cols_a, 2 * pair * H, 2 * H, "hg0" if pair == 2 else None)
-            turned = psum.tile([P, 2, 2, P], F32, tag="work", bufs=3, name="turned")
+            turned = psum.tile([P, 2, 2, P], F32, tag="work", bufs=2, name="turned")
             for b in range(2):
                 slots = slice((2 * pair + b) * P, (2 * pair + b + 1) * P)
                 inner = slice(b * H, (b + 1) * H)
-                acc = psum.tile([P, H], F32, tag="hidden", bufs=2, name="hidden")
-                mx(acc[:], xgw[:, slots], xgs[:, slots], agw[:, inner], ags[:, inner])
+                m = 2 * pair + b
+                if pair < PAIRS - 1:
+                    acc = psum.tile([P, H], F32, tag="hidden", bufs=2, name="hidden")
+                else:
+                    acc = psum.tile([P, H], F32, tag=("y", "total0")[b], bufs=1, name="hidden")
+                mx(acc[:], xgw[:, slots], xgs[:, slots], agw[:, inner], ags[m // 3][:, m % 3 * H : (m % 3 + 1) * H])
                 h = held("h%d" % (2 * pair + b), [P, H], BF16)
                 nc.scalar.activation(
                     h[:].rearrange("j (u p e) -> j u p e", u=2, e=2),
@@ -147,20 +157,19 @@ def tile_moe_dyl_relu_kernel(
             )
             return hg
 
-        def second_matrices(pair):
-            bgw = gather("bgw%d" % pair, wbw, U32, cols_b, 2 * pair * N, 2 * N, "bgw", 2)
-            bgs = gather("bgs%d" % pair, wbs, U8, cols_b, 2 * pair * N, 2 * N, "bgs", 2)
-            return bgw, bgs
+        def second_words(pair):
+            return gather("bgw%d" % pair, wbw, U32, cols_b, 2 * pair * N, 2 * N, "bgw", 2)
 
         def second_layer(pair, hg, bgw, bgs):
             hw = held("hw%d" % pair, [P, 2 * P], U32)
             hs = held("hs%d" % pair, [P, 2 * P], U8)
             nc.vector.quantize_mx(out=hw[:].bitcast(FP8X4), scales=hs[:], in_=hg[:])
-            acc = psum.tile([P, 2, N], F32, tag="work", bufs=3, name="y")
+            acc = psum.tile([P, 2, N], F32, tag="y", bufs=1, name="y")
             gated = held("gated%d" % pair, [P, 2, N], F32)
             for b in range(2):
+                m = 2 * pair + b
                 mx(acc[:, b, :], hw[:, b * P : (b + 1) * P], hs[:, b * P : (b + 1) * P],
-                   bgw[:, b * N : (b + 1) * N], bgs[:, b * N : (b + 1) * N])
+                   bgw[:, b * N : (b + 1) * N], bgs[m // 3][:, m % 3 * N : (m % 3 + 1) * N])
             for b in range(2):
                 m = 2 * pair + b
                 nc.scalar.activation(gated[:, b, :], acc[:, b, :], ACT.Copy, scale=gate_col[:, m : m + 1])
@@ -181,19 +190,19 @@ def tile_moe_dyl_relu_kernel(
             picked = tokens[:, first // 16 : (first + count) // 16]
             nc.vector.tensor_copy(result[c][:].indirect(picked), values[:, c, first : first + count])
 
-        ags0 = first_scales(0)
-        ags1 = first_scales(1)
-        hg0 = first_layer(0, ags0)
-        hg1 = first_layer(1, ags1)
-        second0 = second_matrices(0)
-        ags2 = first_scales(2)
-        second1 = second_matrices(1)
-        second_layer(0, hg0, *second0)
-        hg2 = first_layer(2, ags2)
-        second_layer(1, hg1, *second1)
-        second2 = second_matrices(2)
+        ags = [first_scales(0), first_scales(1)]
+        hg0 = first_layer(0, ags)
+        hg1 = first_layer(1, ags)
+        bgw0 = second_words(0)
+        bgs = [second_scales(0)]
+        bgw1 = second_words(1)
+        second_layer(0, hg0, bgw0, bgs)
+        hg2 = first_layer(2, ags)
+        bgs.append(second_scales(1))
+        second_layer(1, hg1, bgw1, bgs)
+        bgw2 = second_words(2)
         scatter(0, 0)
-        second_layer(2, hg2, *second2)
+        second_layer(2, hg2, bgw2, bgs)
         scatter(0, 1)
         for pair in range(1, PAIRS):
             for c in range(HALVES):

from contextlib import ExitStack

import concourse.mybir as mybir
from concourse.masks import make_identity

K, T, E, B, H, N = 512, 1024, 4, 6, 512, 256
FLOPS = 2 * K * N * T + 2 * 128 * B * (K * H + H * N)

F32 = mybir.dt.float32
BF16 = mybir.dt.bfloat16
I32 = mybir.dt.int32
U32 = mybir.dt.uint32
U16 = mybir.dt.uint16
U8 = mybir.dt.uint8
FP8X4 = mybir.dt.float8_e4m3fn_x4
ACT = mybir.ActivationFunctionType

P = 128
SLOTS = P * B
PAIRS = B // 2
BANK = 512
HALVES = N // P


def tile_moe_dyl_relu_kernel(
    tc, x_words, x_scales, w_words, w_scales, wa_words, wa_scales, wb_words, wb_scales, gate, offs, offs2, offs3, out
):
    nc = tc.nc
    with ExitStack() as ctx:
        keep = ctx.enter_context(tc.tile_pool(name="keep", bufs=1))
        psum = ctx.enter_context(tc.psum_pool(name="psum", bufs=1))

        def held(name, shape, dtype, tag=None, bufs=1):
            return keep.tile(shape, dtype, name=name, tag=tag or name, bufs=bufs, align_bytes=64)

        def plane(name, width):
            tile = held(name, [P, width], U8)
            nc.vector.memset(tile[:].bitcast(I32), 0)
            return tile

        def load_plane(queue, tile, scales):
            for r in range(4):
                queue.dma_start(tile[r:P:32, :].bitcast(I32), scales[0, r:16:4, :].bitcast(I32))

        def load_words(name, words):
            tile = held(name, [P, words.shape[2]], I32)
            nc.sync.dma_start(tile[:], words[0].rearrange("p c d -> p (c d)").bitcast(I32))
            return tile

        def load_list(name, source):
            tile = held(name, [P, source.shape[1]], U16)
            nc.sync.dma_start(tile[:], source)
            return tile

        def mx(result, a_words, a_scales, b_words, b_scales):
            nc.tensor.matmul_mx(
                out=result, lhsT=a_words.bitcast(FP8X4), lhsT_scale=a_scales,
                rhs=b_words.bitcast(FP8X4), rhs_scale=b_scales, start=True, stop=True,
            )

        def gather(name, window, dtype, offsets, first, count, tag=None, bufs=1):
            tile = held(name, [P, count], dtype, tag, bufs)
            picked = offsets[:, first // 16 : (first + count) // 16]
            nc.vector.tensor_copy(tile[:], window[:].bitcast(dtype).indirect(picked))
            return tile

        ident = held("ident", [P, P], F32)
        make_identity(nc, ident[:])

        was = plane("was", E * H)
        ws = plane("ws", N)
        wbs = plane("wbs", E * N)

        tokens = load_list("tokens", offs)
        xs = held("xs", [P, T], U8)
        for q in range(4):
            rows = x_scales[0, 4 * q : 4 * q + 4, :].bitcast(I32)
            queue = nc.scalar if q < 2 else nc.sync
            queue.dma_start(xs[32 * q : 32 * q + 32, :].bitcast(I32), rows.unsqueeze(0).to_broadcast([8, 4, T // 4]))
        xw = load_words("xw", x_words)
        cols_a = load_list("cols_a", offs2)
        load_plane(nc.sync, was, wa_scales)
        ww = load_words("ww", w_words)
        load_plane(nc.sync, ws, w_scales)
        waw = load_words("waw", wa_words)
        cols_b = load_list("cols_b", offs3)
        wbw = load_words("wbw", wb_words)
        load_plane(nc.sync, wbs, wb_scales)
        gate_col = held("gate_col", [P, B], F32)
        with nc.allow_non_contiguous_dma(reason="one gate value a partition"):
            nc.sync.dma_start(gate_col[:], gate[0:1, :].rearrange("o (m p) -> p (o m)", p=P))

        xgs = gather("xgs", xs, U8, tokens, 0, SLOTS)
        xgw = gather("xgw", xw, U32, tokens, 0, SLOTS)

        result = [held("result%d" % c, [P, T], F32) for c in range(HALVES)]

        def frozen_layer(c):
            rows = slice(c * P, (c + 1) * P)
            for t0 in range(0, T, BANK):
                cols = slice(t0, t0 + BANK)
                acc = psum.tile([P, BANK], F32, tag="hidden", bufs=2, name="base")
                mx(acc[:], ww[:, rows], ws[:, rows], xw[:, cols], xs[:, cols])
                nc.scalar.activation(result[c][:, cols], acc[:], ACT.Copy)

        frozen_layer(0)
        sums = []
        for pair in range(PAIRS):
            acc = psum.tile([P, 2, N], F32, tag="work", bufs=2, name="slot_base")
            for b in range(2):
                slots = slice((2 * pair + b) * P, (2 * pair + b + 1) * P)
                mx(acc[:, b, :], xgw[:, slots], xgs[:, slots], ww[:], ws[:])
            staged = held("slot_base%d" % pair, [P, 2, N], F32)
            nc.scalar.copy(staged[:], acc[:])
            total = psum.tile([P, HALVES, 2, P], F32, tag="total%d" % pair, bufs=1, name="total")
            for b in range(2):
                for c in range(HALVES):
                    nc.tensor.matmul(
                        total[:, c, b, :], staged[:, b, c * P : (c + 1) * P], ident[:],
                        start=(b == 0 and c == 0), stop=False, is_transpose=True,
                    )
            sums.append(total)
        frozen_layer(1)

        values = held("values", [P, HALVES, SLOTS], F32)

        def first_scales(trio):
            return gather("ags%d" % trio, was, U8, cols_a, 3 * trio * H, 3 * H)

        def second_scales(trio):
            return gather("bgs%d" % trio, wbs, U8, cols_b, 3 * trio * N, 3 * N, "hs0" if trio == 1 else None)

        def first_layer(pair, ags):
            agw = gather("agw%d" % pair, waw, U32, cols_a, 2 * pair * H, 2 * H, "hg0" if pair == 2 else None)
            turned = psum.tile([P, 2, 2, P], F32, tag="work", bufs=2, name="turned")
            for b in range(2):
                slots = slice((2 * pair + b) * P, (2 * pair + b + 1) * P)
                inner = slice(b * H, (b + 1) * H)
                m = 2 * pair + b
                if pair < PAIRS - 1:
                    acc = psum.tile([P, H], F32, tag="hidden", bufs=2, name="hidden")
                else:
                    acc = psum.tile([P, H], F32, tag=("y", "total0")[b], bufs=1, name="hidden")
                mx(acc[:], xgw[:, slots], xgs[:, slots], agw[:, inner], ags[m // 3][:, m % 3 * H : (m % 3 + 1) * H])
                h = held("h%d" % (2 * pair + b), [P, H], BF16)
                nc.scalar.activation(
                    h[:].rearrange("j (u p e) -> j u p e", u=2, e=2),
                    acc[:].rearrange("j (p u e) -> j u p e", u=2, e=2),
                    ACT.Relu,
                )
                for u in range(2):
                    nc.tensor.transpose(turned[:, b, u, :], h[:].bitcast(F32)[:, u * P : (u + 1) * P], ident[:])
            hg = held("hg%d" % pair, [P, 2 * P * 4], BF16)
            nc.scalar.copy(
                hg[:].bitcast(F32).rearrange("p (b j u) -> p b j u", b=2, u=2),
                turned[:].rearrange("p b u j -> p b j u"),
            )
            return hg

        def second_words(pair):
            return gather("bgw%d" % pair, wbw, U32, cols_b, 2 * pair * N, 2 * N, "bgw", 2)

        def second_layer(pair, hg, bgw, bgs):
            hw = held("hw%d" % pair, [P, 2 * P], U32)
            hs = held("hs%d" % pair, [P, 2 * P], U8)
            nc.vector.quantize_mx(out=hw[:].bitcast(FP8X4), scales=hs[:], in_=hg[:])
            acc = psum.tile([P, 2, N], F32, tag="y", bufs=1, name="y")
            gated = held("gated%d" % pair, [P, 2, N], F32)
            for b in range(2):
                m = 2 * pair + b
                mx(acc[:, b, :], hw[:, b * P : (b + 1) * P], hs[:, b * P : (b + 1) * P],
                   bgw[:, b * N : (b + 1) * N], bgs[m // 3][:, m % 3 * N : (m % 3 + 1) * N])
            for b in range(2):
                m = 2 * pair + b
                nc.scalar.activation(gated[:, b, :], acc[:, b, :], ACT.Copy, scale=gate_col[:, m : m + 1])
            for b in range(2):
                for c in range(HALVES):
                    nc.tensor.matmul(
                        sums[pair][:, c, b, :], gated[:, b, c * P : (c + 1) * P], ident[:],
                        start=False, stop=(b == 1 and c == HALVES - 1), is_transpose=True,
                    )
            for c in range(HALVES):
                nc.scalar.copy(
                    values[:, c, 2 * pair * P : 2 * (pair + 1) * P],
                    sums[pair][:, c, :, :].rearrange("n b j -> n (b j)"),
                )

        def scatter(pair, c):
            first, count = 2 * pair * P, 2 * P
            picked = tokens[:, first // 16 : (first + count) // 16]
            nc.vector.tensor_copy(result[c][:].indirect(picked), values[:, c, first : first + count])

        ags = [first_scales(0), first_scales(1)]
        hg0 = first_layer(0, ags)
        hg1 = first_layer(1, ags)
        bgw0 = second_words(0)
        bgs = [second_scales(0)]
        bgw1 = second_words(1)
        second_layer(0, hg0, bgw0, bgs)
        hg2 = first_layer(2, ags)
        bgs.append(second_scales(1))
        second_layer(1, hg1, bgw1, bgs)
        bgw2 = second_words(2)
        scatter(0, 0)
        second_layer(2, hg2, bgw2, bgs)
        scatter(0, 1)
        for pair in range(1, PAIRS):
            for c in range(HALVES):
                scatter(pair, c)
        nc.sync.dma_start(out[0:P, :], result[0][:])
        nc.sync.dma_start(out[P:N, 0:BANK], result[1][:, 0:BANK])
        nc.scalar.dma_start(out[P:N, BANK:T], result[1][:, BANK:T])
